import numpy as np
import ml_dtypes


def mxq(x, axis, fmt="e4m3"):
    dtype, down = {"e4m3": (ml_dtypes.float8_e4m3fn, 7), "e5m2": (ml_dtypes.float8_e5m2, 14)}[fmt]
    v = np.moveaxis(np.asarray(x, np.float32).astype(ml_dtypes.bfloat16).astype(np.float64), axis, -1)
    blocks = v.reshape(v.shape[:-1] + (-1, 32))
    amax = np.abs(blocks).max(-1, keepdims=True)
    byte = np.maximum(np.where(amax > 0, np.frexp(amax)[1] - 1 + 127, 0) - down, 1)
    scale = np.exp2(byte - 127.0)
    codes = (blocks / scale).astype(np.float32).astype(dtype).astype(np.float64)
    return np.moveaxis((codes * scale).reshape(v.shape), -1, axis)


WIDE = False


def mx_kscale(k):
    if not WIDE:
        return np.ones(k)
    levels = np.array([10, -10, 5, -5, 0])
    if k % 512:
        return np.exp2(np.random.permutation(np.resize(levels, k // 32))).repeat(32)
    a = np.empty((k // 512, 16))
    for p in range(k // 512):
        a[p, :8] = np.random.permutation(np.resize(levels, 8))
        for g in range(8):
            far = levels[np.abs(levels - a[p, g]) >= 10]
            a[p, g + 8] = far[np.random.randint(len(far))]
    return np.exp2(a.ravel()).repeat(32)


BF16 = ml_dtypes.bfloat16


def bf(x):
    return np.asarray(x, np.float32).astype(BF16)


def f64(x):
    return np.asarray(x).astype(np.float64)


E2M1 = np.array([0.0, 0.5, 1.0, 1.5, 2.0, 3.0, 4.0, 6.0, -0.0, -0.5, -1.0, -1.5, -2.0, -3.0, -4.0, -6.0])


def pack_weight(w, fmt):
    k, n = w.shape
    w = f64(bf(w)).reshape(k // 32, 32, n)
    amax = np.abs(w).max(1)
    if fmt == "e4m3":
        byte = np.frexp(amax)[1] - 1 + 127 - 7
    else:
        mant, ex = np.frexp(amax / 6.0)
        byte = np.where(mant > 0.5, ex, ex - 1) + 127
    byte = np.clip(np.where(amax > 0, byte, 1), 1, 254)
    scaled = (w * np.exp2(127.0 - byte)[:, None, :]).reshape(k, n).astype(np.float32)
    by_word = np.ascontiguousarray(scaled.reshape(k // 512, 128, 4, n).transpose(0, 1, 3, 2))
    if fmt == "e4m3":
        words = by_word.astype(ml_dtypes.float8_e4m3fn).view(np.uint8)
    else:
        c = by_word.astype(ml_dtypes.float4_e2m1fn).view(np.uint8) & 0xF
        words = c[..., 0::2] | (c[..., 1::2] << 4)
    return np.ascontiguousarray(words), np.ascontiguousarray(byte.astype(np.uint8).reshape(k // 512, 16, n))


def unpack_weight(words, scales, fmt):
    g, p, n, _ = words.shape
    if fmt == "e4m3":
        vals = np.ascontiguousarray(words).view(ml_dtypes.float8_e4m3fn).astype(np.float64)
    else:
        nib = np.empty((g, p, n, 4), np.uint8)
        nib[..., 0::2] = words & 0xF
        nib[..., 1::2] = words >> 4
        vals = E2M1[nib]
    vals = vals * np.repeat(np.exp2(scales.astype(np.float64) - 127.0), 8, axis=1)[..., None]
    return vals.transpose(0, 1, 3, 2).reshape(g * 512, n)
def pack4(w):
    words, scales = pack_weight(w, "e2m1")
    return words.reshape(words.shape[0], 128, -1), scales


def unpack4(words, scales):
    return unpack_weight(words.reshape(words.shape[0], 128, -1, 2), scales, "e2m1")


M, F, E, D = 1024, 1024, 2048, 1024


def setup_inputs():
    s = mx_kscale(F)
    t = mx_kscale(E)
    h = np.random.standard_normal((M, F)) * s
    v = np.random.standard_normal((M, E)) * t
    r = np.random.uniform(0.4, 1.0, (M,))
    x = np.random.standard_normal((M, D))
    ws = np.random.standard_normal((F, D)) / np.sqrt(F) / s[:, None]
    wr = np.random.standard_normal((E, D)) / np.sqrt(E) / t[:, None]
    wr_words, wr_scales = pack4(wr)
    return {"h": bf(h), "v": bf(v), "r": bf(r), "x": bf(x), "ws": bf(ws),
            "wr_words": wr_words, "wr_scales": wr_scales}


def reference(h, v, r, x, ws, wr_words, wr_scales):
    e = f64(v) * f64(r)[:, None]
    shared = mxq(f64(h), 1, "e4m3") @ mxq(f64(ws), 0, "e4m3")
    routed = mxq(e, 1, "e4m3") @ unpack4(wr_words, wr_scales)
    y = shared + routed + f64(x)
    return y

@@ -1,0 +1,323 @@
+from contextlib import ExitStack
+
+import concourse.mybir as mybir
+from concourse.masks import make_identity
+
+M, F, E, D = 1024, 1024, 2048, 1024
+FLOPS = 2 * M * D * (F + E)
+
+F32 = mybir.dt.float32
+BF16 = mybir.dt.bfloat16
+I32 = mybir.dt.int32
+U32 = mybir.dt.uint32
+U8 = mybir.dt.uint8
+FP8X4 = mybir.dt.float8_e4m3fn_x4
+FP4X4 = mybir.dt.float4_e2m1fn_x4
+
+P = 128
+PACK = 4
+K_PASS = P * PACK
+TILES = M // P
+N_TILE = 512
+PASSES_S = F // K_PASS
+PASSES_R = E // K_PASS
+SPAN = 1024
+SPAN_PASSES = SPAN // K_PASS
+BANKS = 8
+WS_CUT = 256
+
+
+def tile_shared_routed_expert_pair_s1_kernel(tc, h, v, r, x, ws, wr_words, wr_scales, out):
+    nc = tc.nc
+    h_rows = h.rearrange("(p i) k -> p i k", i=TILES)
+    v_rows = v.rearrange("(p i) k -> p i k", i=TILES)
+    x_rows = x.rearrange("(p i) n -> p i n", i=TILES)
+    out_rows = out.rearrange("(p i) n -> p i n", i=TILES)
+
+    with ExitStack() as ctx:
+        keep = ctx.enter_context(tc.tile_pool(name="keep", bufs=1))
+        stage = ctx.enter_context(tc.tile_pool(name="stage", bufs=6))
+        psum = ctx.enter_context(tc.psum_pool(name="psum", bufs=1))
+        ctx.enter_context(tc.manual_schedule())
+
+        ident = keep.tile([P, P], F32, name="ident")
+        make_identity(nc, ident[:])
+
+        wr_sc = keep.tile([P, PASSES_R, D], U8, name="wr_sc", align_bytes=64)
+        nc.vector.memset(wr_sc[:].rearrange("p g n -> p (g n)").bitcast(I32), 0)
+
+        r_sb = keep.tile([P, TILES], BF16, name="r_sb")
+        raw, x_sb, wr_sb, ws_raw = {}, {}, {}, {}
+
+        def load_v(i):
+            rows = keep.tile([P, E], BF16, name="v%d" % i)
+            nc.sync.dma_start(out=rows[:], in_=v_rows[:, i, :])
+            for s in range(2):
+                raw["v", i, s] = rows[:, s * SPAN : (s + 1) * SPAN]
+
+        def load_v_span(i, s):
+            rows = keep.tile([P, SPAN], BF16, name="v%d_%d" % (i, s))
+            nc.sync.dma_start(out=rows[:], in_=v_rows[:, i, s * SPAN : (s + 1) * SPAN])
+            raw["v", i, s] = rows[:]
+
+        def load_h(first, count):
+            rows = keep.tile([P, count * F], BF16, name="h%d" % first)
+            nc.sync.dma_start(out=rows[:], in_=h_rows[:, first : first + count, :].rearrange("p i k -> p (i k)"))
+            for c in range(count):
+                raw["h", first + c, 0] = rows[:, c * F : (c + 1) * F]
+
+        def load_x(first, count, halves):
+            cols = slice(halves[0] * N_TILE, (halves[-1] + 1) * N_TILE)
+            rows = keep.tile([P, count, len(halves) * N_TILE], BF16, name="x%d_%d" % (first, halves[0]))
+            nc.sync.dma_start(out=rows[:], in_=x_rows[:, first : first + count, cols])
+            for c in range(count):
+                for j, n in enumerate(halves):
+                    x_sb[first + c, n] = rows[:, c, j * N_TILE : (j + 1) * N_TILE]
+
+        def load_wr(g):
+            wr_sb[g] = keep.tile([P, 2 * D], U8, name="wr%d" % g, align_bytes=64)
+            nc.sync.dma_start(out=wr_sb[g][:].bitcast(I32), in_=wr_words[g].bitcast(I32))
+
+        def load_wr_scales():
+            by_row = wr_scales.rearrange("g (q s) n -> s q g n", s=4)
+            for s in range(4):
+                nc.sync.dma_start(out=wr_sc[s:P:32, :, :].bitcast(I32), in_=by_row[s].bitcast(I32))
+
+        def load_ws(g, n):
+            ws_raw[g, n] = keep.tile([P, PACK, N_TILE], BF16, name="ws%d_%d" % (g, n))
+            src = ws[g * K_PASS : (g + 1) * K_PASS, n * N_TILE : (n + 1) * N_TILE]
+            nc.sync.dma_start(out=ws_raw[g, n][:], in_=src.rearrange("(p j) n -> p j n", j=PACK))
+
+        free_banks = list(range(BANKS))
+
+        def take_bank():
+            b = free_banks[0]
+            free_banks.remove(b)
+            return b
+
+        ordered, turned, grouped, quantised, ws_grouped, acc = {}, {}, {}, {}, {}, {}
+
+        def sort(*keys):
+            for key in keys:
+                ordered[key] = stage.tile([P, 2, SPAN // 2], BF16, name="ordered")
+                dst = ordered[key][:].rearrange("p u (w e) -> p u w e", e=2)
+                src = raw[key].rearrange("p (w u e) -> p u w e", u=2, e=2)
+                if key[0] == "v":
+                    i = key[1]
+                    nc.vector.tensor_scalar(
+                        out=dst, in0=src, scalar1=r_sb[:, i : i + 1], scalar2=None, op0=mybir.AluOpType.mult
+                    )
+                else:
+                    nc.vector.tensor_copy(out=dst, in_=src)
+
+        def turn(*keys):
+            for key in keys:
+                words = ordered[key][:].bitcast(F32)
+                b = take_bank()
+                bank = psum.tile([P, SPAN_PASSES, 2, P], F32, name="turned", tag="bank%d" % b)
+                for g in range(SPAN_PASSES):
+                    for u in range(2):
+                        nc.tensor.transpose(bank[:, g, u, :], words[:, u, g * P : (g + 1) * P], ident[:])
+                turned[key] = (b, bank)
+
+        def regroup(*keys):
+            for key in keys:
+                b, bank = turned[key]
+                grouped[key] = stage.tile([P, SPAN], BF16, name="grouped", align_bytes=64)
+                words = grouped[key][:].bitcast(F32).rearrange("p (g t u) -> p g t u", t=P, u=2)
+                nc.scalar.copy(out=words, in_=bank[:].rearrange("p g u t -> p g t u"))
+                free_banks.append(b)
+
+        def quantize(key, src):
+            width = src.shape[1] // PACK
+            name = "%s%d_%d" % key
+            codes = keep.tile([P, width], U32, name=name + "_codes", align_bytes=64)
+            scales = keep.tile([P, width], U8, name=name + "_scales", align_bytes=64)
+            nc.vector.quantize_mx(out=codes[:].bitcast(FP8X4), scales=scales[:], in_=src[:])
+            quantised[key] = (codes, scales)
+
+        def quant(*keys):
+            for key in keys:
+                quantize(key, grouped[key])
+
+        def group_ws(g, n, cut):
+            ws_grouped[g, n] = keep.tile([P, PACK * N_TILE], BF16, name="wsg%d_%d" % (g, n), align_bytes=64)
+            dst = ws_grouped[g, n][:].rearrange("p (c j) -> p c j", j=PACK)
+            src = ws_raw[g, n][:].rearrange("p j c -> p c j")
+            nc.scalar.copy(out=dst[:, :cut, :], in_=src[:, :cut, :])
+            if cut < N_TILE:
+                nc.vector.tensor_copy(out=dst[:, cut:, :], in_=src[:, cut:, :])
+
+        def quant_ws(g, n):
+            quantize(("ws", g, n), ws_grouped[g, n])
+
+        def stationary(kind, i, g):
+            codes, scales = quantised[kind, i, g // SPAN_PASSES]
+            cols = slice((g % SPAN_PASSES) * P, (g % SPAN_PASSES + 1) * P)
+            return codes[:, cols].bitcast(FP8X4), scales[:, cols]
+
+        def routed(i, n, passes=range(PASSES_R)):
+            for g in passes:
+                if g == 0:
+                    b = take_bank()
+                    acc[i, n] = (b, psum.tile([P, N_TILE], F32, name="acc", tag="bank%d" % b))
+                codes, scales = stationary("v", i, g)
+                nc.tensor.matmul_mx(
+                    out=acc[i, n][1][:],
+                    lhsT=codes,
+                    lhsT_scale=scales,
+                    rhs=wr_sb[g][:, 2 * n * N_TILE : 2 * (n + 1) * N_TILE].bitcast(FP4X4),
+                    rhs_scale=wr_sc[:, g, n * N_TILE : (n + 1) * N_TILE],
+                    start=(g == 0),
+                    stop=False,
+                )
+
+        def shared(i, n, passes=range(PASSES_S)):
+            for g in passes:
+                codes, scales = stationary("h", i, g)
+                w_codes, w_scales = quantised["ws", g, n]
+                nc.tensor.matmul_mx(
+                    out=acc[i, n][1][:],
+                    lhsT=codes,
+                    lhsT_scale=scales,
+                    rhs=w_codes[:].bitcast(FP8X4),
+                    rhs_scale=w_scales[:],
+                    start=False,
+                    stop=(g == PASSES_S - 1),
+                )
+
+        def add_x(i, n):
+            b, bank = acc[i, n]
+            y = keep.tile([P, N_TILE], F32, name="y%d_%d" % (i, n))
+            nc.vector.tensor_tensor(out=y[:], in0=bank[:], in1=x_sb[i, n], op=mybir.AluOpType.add)
+            free_banks.append(b)
+            nc.sync.dma_start(out=out_rows[:, i, n * N_TILE : (n + 1) * N_TILE], in_=y[:])
+
+        def v_spans(i):
+            return ("v", i, 0), ("v", i, 1)
+
+        def spans(i):
+            return ("v", i, 0), ("v", i, 1), ("h", i, 0)
+
+        nc.sync.dma_start(out=r_sb[:], in_=r.rearrange("(p i) -> p i", i=TILES))
+        for s in range(2):
+            for i in range(2):
+                load_v_span(i, s)
+        load_wr_scales()
+        load_wr(0)
+        load_wr(1)
+        load_v(2)
+        load_wr(2)
+        load_wr(3)
+        load_ws(0, 0)
+        load_h(0, 2)
+        load_ws(1, 0)
+        load_v(3)
+        load_h(2, 2)
+        load_x(0, 4, [0])
+        load_v(4)
+        load_h(4, 2)
+        load_ws(0, 1)
+        load_v(5)
+        load_ws(1, 1)
+        load_x(4, 2, [0])
+        load_x(0, 6, [1])
+        load_v(6)
+        load_h(6, 2)
+        load_v(7)
+        load_x(6, 2, [0, 1])
+
+        def hs(i):
+            return ("h", i, 0), ("h", i + 1, 0)
+
+        early = [("v", i, s) for s in range(2) for i in range(2)]
+        sort(*early)
+        turn(*early)
+        regroup(*early)
+        quant(*early)
+        sort(*v_spans(2))
+        for g in range(PASSES_R):
+            if g == 2:
+                turn(*v_spans(2))
+                regroup(*v_spans(2))
+                quant(*v_spans(2))
+            for i in range(2):
+                for n in range(2):
+                    routed(i, n, [g])
+        group_ws(0, 0, WS_CUT)
+        sort(*hs(0))
+        routed(2, 0)
+        turn(*hs(0))
+        quant_ws(0, 0)
+        group_ws(1, 0, WS_CUT)
+        regroup(*hs(0))
+        routed(2, 1)
+        sort(*v_spans(3))
+        turn(*v_spans(3))
+        regroup(*v_spans(3))
+        quant(("h", 0, 0))
+        quant_ws(1, 0)
+        quant(("h", 1, 0))
+        shared(0, 0)
+        shared(1, 0)
+        sort(*hs(2))
+        add_x(0, 0)
+        quant(*v_spans(3))
+        turn(*hs(2))
+        regroup(*hs(2))
+        routed(3, 0)
+        sort(*v_spans(4))
+        add_x(1, 0)
+        quant(*hs(2))
+        turn(*v_spans(4))
+        regroup(*v_spans(4))
+        shared(2, 0)
+        shared(3, 0)
+        sort(*hs(4))
+        quant(*v_spans(4))
+        turn(*hs(4))
+        regroup(*hs(4))
+        add_x(2, 0)
+        routed(4, 0)
+        sort(*v_spans(5))
+        group_ws(0, 1, WS_CUT)
+        add_x(3, 0)
+        quant(*hs(4))
+        turn(*v_spans(5))
+        regroup(*v_spans(5))
+        routed(3, 1)
+        quant_ws(0, 1)
+        group_ws(1, 1, WS_CUT)
+        shared(4, 0)
+        quant(*v_spans(5))
+        routed(4, 1)
+        add_x(4, 0)
+        quant_ws(1, 1)
+        routed(5, 0)
+        shared(5, 0)
+        sort(*v_spans(6))
+        sort(*hs(6))
+        for i in range(5):
+            shared(i, 1)
+        add_x(5, 0)
+        add_x(0, 1)
+        add_x(1, 1)
+        turn(*spans(6))
+        regroup(*spans(6))
+        add_x(2, 1)
+        sort(*v_spans(7))
+        routed(5, 1)
+        shared(5, 1)
+        quant(*spans(6))
+        add_x(3, 1)
+        add_x(4, 1)
+        turn(*spans(7))
+        regroup(*spans(7))
+        add_x(5, 1)
+        for i in range(6, TILES):
+            for n in range(2):
+                routed(i, n)
+                shared(i, n)
+                if (i, n) == (6, 0):
+                    quant(*spans(7))
+                add_x(i, n)

@@ -24,7 +24,8 @@ PASSES_R = E // K_PASS
 SPAN = 1024
 SPAN_PASSES = SPAN // K_PASS
 BANKS = 8
-WS_CUT = 256
+RUN = 4
+WS_CUT = 128
 
 
 def tile_shared_routed_expert_pair_s1_kernel(tc, h, v, r, x, ws, wr_words, wr_scales, out):
@@ -36,7 +37,7 @@ def tile_shared_routed_expert_pair_s1_kernel(tc, h, v, r, x, ws, wr_words, wr_sc
 
     with ExitStack() as ctx:
         keep = ctx.enter_context(tc.tile_pool(name="keep", bufs=1))
-        stage = ctx.enter_context(tc.tile_pool(name="stage", bufs=6))
+        stage = ctx.enter_context(tc.tile_pool(name="stage", bufs=4))
         psum = ctx.enter_context(tc.psum_pool(name="psum", bufs=1))
         ctx.enter_context(tc.manual_schedule())
 
@@ -49,22 +50,15 @@ def tile_shared_routed_expert_pair_s1_kernel(tc, h, v, r, x, ws, wr_words, wr_sc
         r_sb = keep.tile([P, TILES], BF16, name="r_sb")
         raw, x_sb, wr_sb, ws_raw = {}, {}, {}, {}
 
-        def load_v(i):
-            rows = keep.tile([P, E], BF16, name="v%d" % i)
-            nc.sync.dma_start(out=rows[:], in_=v_rows[:, i, :])
-            for s in range(2):
-                raw["v", i, s] = rows[:, s * SPAN : (s + 1) * SPAN]
+        def load_v(i, first=0, count=2):
+            rows = keep.tile([P, count * SPAN], BF16, name="v%d_%d" % (i, first))
+            nc.sync.dma_start(out=rows[:], in_=v_rows[:, i, first * SPAN : (first + count) * SPAN])
+            raw["v", i, first] = rows
 
-        def load_v_span(i, s):
-            rows = keep.tile([P, SPAN], BF16, name="v%d_%d" % (i, s))
-            nc.sync.dma_start(out=rows[:], in_=v_rows[:, i, s * SPAN : (s + 1) * SPAN])
-            raw["v", i, s] = rows[:]
-
-        def load_h(first, count):
-            rows = keep.tile([P, count * F], BF16, name="h%d" % first)
-            nc.sync.dma_start(out=rows[:], in_=h_rows[:, first : first + count, :].rearrange("p i k -> p (i k)"))
-            for c in range(count):
-                raw["h", first + c, 0] = rows[:, c * F : (c + 1) * F]
+        def load_h(i):
+            rows = keep.tile([P, 2 * F], BF16, name="h%d" % i)
+            nc.sync.dma_start(out=rows[:], in_=h_rows[:, i : i + 2, :].rearrange("p i k -> p (i k)"))
+            raw["h", i, 0] = rows
 
         def load_x(first, count, halves):
             cols = slice(halves[0] * N_TILE, (halves[-1] + 1) * N_TILE)
@@ -95,229 +89,259 @@ def tile_shared_routed_expert_pair_s1_kernel(tc, h, v, r, x, ws, wr_words, wr_sc
             free_banks.remove(b)
             return b
 
-        ordered, turned, grouped, quantised, ws_grouped, acc = {}, {}, {}, {}, {}, {}
+        ordered, turned, grouped, lhs, ws_grouped, ws_q, acc = {}, {}, {}, {}, {}, {}, {}
 
-        def sort(*keys):
+        def sort(*keys, on_scalar=False):
             for key in keys:
-                ordered[key] = stage.tile([P, 2, SPAN // 2], BF16, name="ordered")
+                width = raw[key].shape[1]
+                ordered[key] = stage.tile([P, 2, width // 2], BF16, name="ordered")
                 dst = ordered[key][:].rearrange("p u (w e) -> p u w e", e=2)
-                src = raw[key].rearrange("p (w u e) -> p u w e", u=2, e=2)
+                src = raw[key][:].rearrange("p (w u e) -> p u w e", u=2, e=2)
                 if key[0] == "v":
                     i = key[1]
                     nc.vector.tensor_scalar(
                         out=dst, in0=src, scalar1=r_sb[:, i : i + 1], scalar2=None, op0=mybir.AluOpType.mult
                     )
+                elif on_scalar:
+                    words = raw[key][:].bitcast(F32).rearrange("p (w u) -> p u w", u=2)
+                    nc.scalar.copy(out=ordered[key][:].bitcast(F32), in_=words)
                 else:
                     nc.vector.tensor_copy(out=dst, in_=src)
 
         def turn(*keys):
             for key in keys:
                 words = ordered[key][:].bitcast(F32)
-                b = take_bank()
-                bank = psum.tile([P, SPAN_PASSES, 2, P], F32, name="turned", tag="bank%d" % b)
-                for g in range(SPAN_PASSES):
-                    for u in range(2):
-                        nc.tensor.transpose(bank[:, g, u, :], words[:, u, g * P : (g + 1) * P], ident[:])
-                turned[key] = (b, bank)
+                turned[key] = []
+                for s in range(raw[key].shape[1] // SPAN):
+                    b = take_bank()
+                    bank = psum.tile([P, SPAN_PASSES, 2, P], F32, name="turned", tag="bank%d" % b)
+                    for j in range(SPAN_PASSES):
+                        g = s * SPAN_PASSES + j
+                        for u in range(2):
+                            nc.tensor.transpose(bank[:, j, u, :], words[:, u, g * P : (g + 1) * P], ident[:])
+                    turned[key].append((b, bank))
 
         def regroup(*keys):
             for key in keys:
-                b, bank = turned[key]
-                grouped[key] = stage.tile([P, SPAN], BF16, name="grouped", align_bytes=64)
+                grouped[key] = stage.tile([P, raw[key].shape[1]], BF16, name="grouped", align_bytes=64)
                 words = grouped[key][:].bitcast(F32).rearrange("p (g t u) -> p g t u", t=P, u=2)
-                nc.scalar.copy(out=words, in_=bank[:].rearrange("p g u t -> p g t u"))
-                free_banks.append(b)
+                for s, (b, bank) in enumerate(turned[key]):
+                    dst = words[:, s * SPAN_PASSES : (s + 1) * SPAN_PASSES, :, :]
+                    nc.scalar.copy(out=dst, in_=bank[:].rearrange("p g u t -> p g t u"))
+                    free_banks.append(b)
 
-        def quantize(key, src):
+        def quantize(name, src):
             width = src.shape[1] // PACK
-            name = "%s%d_%d" % key
             codes = keep.tile([P, width], U32, name=name + "_codes", align_bytes=64)
             scales = keep.tile([P, width], U8, name=name + "_scales", align_bytes=64)
             nc.vector.quantize_mx(out=codes[:].bitcast(FP8X4), scales=scales[:], in_=src[:])
-            quantised[key] = (codes, scales)
+            return codes, scales
 
-        def quant(*keys):
-            for key in keys:
-                quantize(key, grouped[key])
+        def quant(key, spans=None):
+            kind, i, first = key
+            if spans is None:
+                spans = range(raw[key].shape[1] // SPAN)
+            src = grouped[key][:, spans[0] * SPAN : (spans[-1] + 1) * SPAN]
+            codes, scales = quantize("%s%d_%d" % (kind, i, first + spans[0]), src)
+            for c in range(codes.shape[1] // P):
+                cols = slice(c * P, (c + 1) * P)
+                g = (first + spans[0]) * SPAN_PASSES + c
+                where = (kind, i, g) if kind == "v" else (kind, i + g // PASSES_S, g % PASSES_S)
+                lhs[where] = (codes[:, cols].bitcast(FP8X4), scales[:, cols])
 
-        def group_ws(g, n, cut):
-            ws_grouped[g, n] = keep.tile([P, PACK * N_TILE], BF16, name="wsg%d_%d" % (g, n), align_bytes=64)
-            dst = ws_grouped[g, n][:].rearrange("p (c j) -> p c j", j=PACK)
-            src = ws_raw[g, n][:].rearrange("p j c -> p c j")
-            nc.scalar.copy(out=dst[:, :cut, :], in_=src[:, :cut, :])
-            if cut < N_TILE:
-                nc.vector.tensor_copy(out=dst[:, cut:, :], in_=src[:, cut:, :])
+        def group_ws(engine_copy, g, n, first, last):
+            if (g, n) not in ws_grouped:
+                ws_grouped[g, n] = keep.tile([P, PACK * N_TILE], BF16, name="wsg%d_%d" % (g, n), align_bytes=64)
+            dst = ws_grouped[g, n][:].rearrange("p (c i j) -> p c j i", i=RUN, j=PACK)
+            src = ws_raw[g, n][:].rearrange("p j (c i) -> p c j i", i=RUN)
+            runs = slice(first // RUN, last // RUN)
+            engine_copy(out=dst[:, runs, :, :], in_=src[:, runs, :, :])
+
+        def group_ws_shared(g, n):
+            group_ws(nc.scalar.copy, g, n, 0, WS_CUT)
+            group_ws(nc.vector.tensor_copy, g, n, WS_CUT, N_TILE)
 
         def quant_ws(g, n):
-            quantize(("ws", g, n), ws_grouped[g, n])
+            ws_q[g, n] = quantize("ws%d_%d" % (g, n), ws_grouped[g, n])
 
-        def stationary(kind, i, g):
-            codes, scales = quantised[kind, i, g // SPAN_PASSES]
-            cols = slice((g % SPAN_PASSES) * P, (g % SPAN_PASSES + 1) * P)
-            return codes[:, cols].bitcast(FP8X4), scales[:, cols]
-
-        def routed(i, n, passes=range(PASSES_R)):
+        def routed(i, cols, passes=range(PASSES_R)):
+            first, width = cols
             for g in passes:
                 if g == 0:
                     b = take_bank()
-                    acc[i, n] = (b, psum.tile([P, N_TILE], F32, name="acc", tag="bank%d" % b))
-                codes, scales = stationary("v", i, g)
+                    acc[i, cols] = (b, psum.tile([P, width], F32, name="acc", tag="bank%d" % b))
+                codes, scales = lhs["v", i, g]
                 nc.tensor.matmul_mx(
-                    out=acc[i, n][1][:],
+                    out=acc[i, cols][1][:],
                     lhsT=codes,
                     lhsT_scale=scales,
-                    rhs=wr_sb[g][:, 2 * n * N_TILE : 2 * (n + 1) * N_TILE].bitcast(FP4X4),
-                    rhs_scale=wr_sc[:, g, n * N_TILE : (n + 1) * N_TILE],
+                    rhs=wr_sb[g][:, 2 * first : 2 * (first + width)].bitcast(FP4X4),
+                    rhs_scale=wr_sc[:, g, first : first + width],
                     start=(g == 0),
                     stop=False,
                 )
 
-        def shared(i, n, passes=range(PASSES_S)):
-            for g in passes:
-                codes, scales = stationary("h", i, g)
-                w_codes, w_scales = quantised["ws", g, n]
+        def shared(i, cols):
+            first, width = cols
+            n, within = divmod(first, N_TILE)
+            for g in range(PASSES_S):
+                codes, scales = lhs["h", i, g]
+                w_codes, w_scales = ws_q[g, n]
                 nc.tensor.matmul_mx(
-                    out=acc[i, n][1][:],
+                    out=acc[i, cols][1][:],
                     lhsT=codes,
                     lhsT_scale=scales,
-                    rhs=w_codes[:].bitcast(FP8X4),
-                    rhs_scale=w_scales[:],
+                    rhs=w_codes[:, within : within + width].bitcast(FP8X4),
+                    rhs_scale=w_scales[:, within : within + width],
                     start=False,
                     stop=(g == PASSES_S - 1),
                 )
 
-        def add_x(i, n):
-            b, bank = acc[i, n]
-            y = keep.tile([P, N_TILE], F32, name="y%d_%d" % (i, n))
-            nc.vector.tensor_tensor(out=y[:], in0=bank[:], in1=x_sb[i, n], op=mybir.AluOpType.add)
+        def add_x(i, cols):
+            first, width = cols
+            n, within = divmod(first, N_TILE)
+            b, bank = acc[i, cols]
+            y = keep.tile([P, width], F32, name="y%d_%d" % (i, first))
+            nc.vector.tensor_tensor(
+                out=y[:], in0=bank[:], in1=x_sb[i, n][:, within : within + width], op=mybir.AluOpType.add
+            )
             free_banks.append(b)
-            nc.sync.dma_start(out=out_rows[:, i, n * N_TILE : (n + 1) * N_TILE], in_=y[:])
+            nc.sync.dma_start(out=out_rows[:, i, first : first + width], in_=y[:])
 
-        def v_spans(i):
-            return ("v", i, 0), ("v", i, 1)
+        def both(i, cols):
+            routed(i, cols)
+            shared(i, cols)
 
-        def spans(i):
-            return ("v", i, 0), ("v", i, 1), ("h", i, 0)
+        left, right = (0, N_TILE), (N_TILE, N_TILE)
 
         nc.sync.dma_start(out=r_sb[:], in_=r.rearrange("(p i) -> p i", i=TILES))
-        for s in range(2):
-            for i in range(2):
-                load_v_span(i, s)
+        early = [("v", i, s) for s in range(2) for i in range(2)]
+        for kind, i, s in early:
+            load_v(i, s, 1)
         load_wr_scales()
         load_wr(0)
         load_wr(1)
-        load_v(2)
-        load_wr(2)
-        load_wr(3)
         load_ws(0, 0)
-        load_h(0, 2)
+        load_wr(2)
+        load_v(2)
+        load_wr(3)
+        load_h(0)
         load_ws(1, 0)
         load_v(3)
-        load_h(2, 2)
-        load_x(0, 4, [0])
+        load_x(0, 2, [0])
+        load_h(2)
         load_v(4)
-        load_h(4, 2)
+        load_x(2, 4, [0])
+        load_h(4)
         load_ws(0, 1)
         load_v(5)
         load_ws(1, 1)
-        load_x(4, 2, [0])
         load_x(0, 6, [1])
         load_v(6)
-        load_h(6, 2)
+        load_h(6)
         load_v(7)
         load_x(6, 2, [0, 1])
 
-        def hs(i):
-            return ("h", i, 0), ("h", i + 1, 0)
+        v_of = [("v", i, 0) for i in range(TILES)]
+        h_of = [("h", i, 0) for i in range(TILES)]
+        half = N_TILE // 2
 
-        early = [("v", i, s) for s in range(2) for i in range(2)]
         sort(*early)
         turn(*early)
         regroup(*early)
-        quant(*early)
-        sort(*v_spans(2))
-        for g in range(PASSES_R):
-            if g == 2:
-                turn(*v_spans(2))
-                regroup(*v_spans(2))
-                quant(*v_spans(2))
-            for i in range(2):
-                for n in range(2):
-                    routed(i, n, [g])
-        group_ws(0, 0, WS_CUT)
-        sort(*hs(0))
-        routed(2, 0)
-        turn(*hs(0))
+        for key in early:
+            quant(key)
+        group_ws(nc.scalar.copy, 0, 0, 0, N_TILE)
+        sort(v_of[2])
         quant_ws(0, 0)
-        group_ws(1, 0, WS_CUT)
-        regroup(*hs(0))
-        routed(2, 1)
-        sort(*v_spans(3))
-        turn(*v_spans(3))
-        regroup(*v_spans(3))
-        quant(("h", 0, 0))
+        sort(h_of[0])
+        for g in range(PASSES_R):
+            if g == PASSES_R - 1:
+                turn(v_of[2])
+                regroup(v_of[2])
+            for i in range(2):
+                routed(i, left, [g])
+                routed(i, right, [g])
+        turn(h_of[0])
+        quant(v_of[2], [0])
+        quant(v_of[2], [1])
+        group_ws(nc.scalar.copy, 1, 0, 0, WS_CUT)
+        group_ws(nc.vector.tensor_copy, 1, 0, WS_CUT, N_TILE)
+        regroup(h_of[0])
+        routed(2, left)
+        routed(2, right)
+        sort(v_of[3])
+        quant(h_of[0])
+        sort(h_of[2], on_scalar=True)
         quant_ws(1, 0)
-        quant(("h", 1, 0))
-        shared(0, 0)
-        shared(1, 0)
-        sort(*hs(2))
-        add_x(0, 0)
-        quant(*v_spans(3))
-        turn(*hs(2))
-        regroup(*hs(2))
-        routed(3, 0)
-        sort(*v_spans(4))
-        add_x(1, 0)
-        quant(*hs(2))
-        turn(*v_spans(4))
-        regroup(*v_spans(4))
-        shared(2, 0)
-        shared(3, 0)
-        sort(*hs(4))
-        quant(*v_spans(4))
-        turn(*hs(4))
-        regroup(*hs(4))
-        add_x(2, 0)
-        routed(4, 0)
-        sort(*v_spans(5))
-        group_ws(0, 1, WS_CUT)
-        add_x(3, 0)
-        quant(*hs(4))
-        turn(*v_spans(5))
-        regroup(*v_spans(5))
-        routed(3, 1)
+        turn(v_of[3])
+        regroup(v_of[3])
+        shared(0, left)
+        shared(1, left)
+        quant(v_of[3], [0])
+        add_x(0, left)
+        quant(v_of[3], [1])
+        turn(h_of[2])
+        regroup(h_of[2])
+        routed(3, left)
+        sort(v_of[4])
+        add_x(1, left)
+        quant(h_of[2], [0])
+        quant(h_of[2], [1])
+        sort(h_of[4], on_scalar=True)
+        turn(v_of[4])
+        regroup(v_of[4])
+        shared(2, left)
+        shared(3, left)
+        group_ws(nc.vector.tensor_copy, 0, 1, half, N_TILE)
+        quant(v_of[4], [0])
+        add_x(2, left)
+        quant(v_of[4], [1])
+        turn(h_of[4])
+        regroup(h_of[4])
+        routed(4, left)
+        sort(v_of[5])
+        group_ws(nc.scalar.copy, 0, 1, 0, half)
+        add_x(3, left)
+        turn(v_of[5])
+        regroup(v_of[5])
+        quant(h_of[4])
+        routed(3, right)
         quant_ws(0, 1)
-        group_ws(1, 1, WS_CUT)
-        shared(4, 0)
-        quant(*v_spans(5))
-        routed(4, 1)
-        add_x(4, 0)
+        group_ws(nc.scalar.copy, 1, 1, 0, N_TILE - WS_CUT)
+        group_ws(nc.vector.tensor_copy, 1, 1, N_TILE - WS_CUT, N_TILE)
+        shared(4, left)
+        quant(v_of[5])
+        routed(4, right)
+        add_x(4, left)
+        sort(v_of[6])
         quant_ws(1, 1)
-        routed(5, 0)
-        shared(5, 0)
-        sort(*v_spans(6))
-        sort(*hs(6))
+        both(5, left)
+        sort(h_of[6], on_scalar=True)
         for i in range(5):
-            shared(i, 1)
-        add_x(5, 0)
-        add_x(0, 1)
-        add_x(1, 1)
-        turn(*spans(6))
-        regroup(*spans(6))
-        add_x(2, 1)
-        sort(*v_spans(7))
-        routed(5, 1)
-        shared(5, 1)
-        quant(*spans(6))
-        add_x(3, 1)
-        add_x(4, 1)
-        turn(*spans(7))
-        regroup(*spans(7))
-        add_x(5, 1)
-        for i in range(6, TILES):
-            for n in range(2):
-                routed(i, n)
-                shared(i, n)
-                if (i, n) == (6, 0):
-                    quant(*spans(7))
-                add_x(i, n)
+            shared(i, right)
+        add_x(5, left)
+        add_x(0, right)
+        add_x(1, right)
+        turn(v_of[6], h_of[6])
+        regroup(v_of[6], h_of[6])
+        add_x(2, right)
+        sort(v_of[7])
+        both(5, right)
+        quant(v_of[6], [0])
+        quant(v_of[6], [1])
+        add_x(3, right)
+        quant(h_of[6])
+        add_x(4, right)
+        turn(v_of[7])
+        regroup(v_of[7])
+        add_x(5, right)
+        both(6, left)
+        quant(v_of[7])
+        add_x(6, left)
+        for i, cols in [(6, right), (7, left)]:
+            both(i, cols)
+            add_x(i, cols)
+        for first in range(N_TILE, D, P):
+            both(7, (first, P))
+            add_x(7, (first, P))

@@ -25,7 +25,6 @@ SPAN = 1024
 SPAN_PASSES = SPAN // K_PASS
 BANKS = 8
 RUN = 4
-WS_CUT = 128
 
 
 def tile_shared_routed_expert_pair_s1_kernel(tc, h, v, r, x, ws, wr_words, wr_scales, out):
@@ -45,28 +44,27 @@ def tile_shared_routed_expert_pair_s1_kernel(tc, h, v, r, x, ws, wr_words, wr_sc
         make_identity(nc, ident[:])
 
         wr_sc = keep.tile([P, PASSES_R, D], U8, name="wr_sc", align_bytes=64)
-        nc.vector.memset(wr_sc[:].rearrange("p g n -> p (g n)").bitcast(I32), 0)
+        warm_in = keep.tile([P, K_PASS], BF16, name="warm_in", align_bytes=64)
+        nc.vector.memset(warm_in[:], 1.0)
 
         r_sb = keep.tile([P, TILES], BF16, name="r_sb")
-        raw, x_sb, wr_sb, ws_raw = {}, {}, {}, {}
+        sheet_sb, x_sb, wr_sb, ws_raw = {}, {}, {}, {}
 
-        def load_v(i, first=0, count=2):
-            rows = keep.tile([P, count * SPAN], BF16, name="v%d_%d" % (i, first))
-            nc.sync.dma_start(out=rows[:], in_=v_rows[:, i, first * SPAN : (first + count) * SPAN])
-            raw["v", i, first] = rows
+        def load_v(i):
+            sheet_sb["v", i] = keep.tile([P, 2 * SPAN], BF16, name="v%d" % i)
+            nc.sync.dma_start(out=sheet_sb["v", i][:], in_=v_rows[:, i, :])
 
         def load_h(i):
-            rows = keep.tile([P, 2 * F], BF16, name="h%d" % i)
-            nc.sync.dma_start(out=rows[:], in_=h_rows[:, i : i + 2, :].rearrange("p i k -> p (i k)"))
-            raw["h", i, 0] = rows
+            sheet_sb["h", i] = keep.tile([P, 2 * SPAN], BF16, name="h%d" % i)
+            nc.sync.dma_start(out=sheet_sb["h", i][:], in_=h_rows[:, i : i + 2, :].rearrange("p i k -> p (i k)"))
 
-        def load_x(first, count, halves):
-            cols = slice(halves[0] * N_TILE, (halves[-1] + 1) * N_TILE)
-            rows = keep.tile([P, count, len(halves) * N_TILE], BF16, name="x%d_%d" % (first, halves[0]))
-            nc.sync.dma_start(out=rows[:], in_=x_rows[:, first : first + count, cols])
+        def load_x(first, count, cols):
+            start, width = cols
+            rows = keep.tile([P, count, width], BF16, name="x%d_%d" % (first, start))
+            nc.sync.dma_start(out=rows[:], in_=x_rows[:, first : first + count, start : start + width])
             for c in range(count):
-                for j, n in enumerate(halves):
-                    x_sb[first + c, n] = rows[:, c, j * N_TILE : (j + 1) * N_TILE]
+                for j in range(width // N_TILE):
+                    x_sb[first + c, start // N_TILE + j] = rows[:, c, j * N_TILE : (j + 1) * N_TILE]
 
         def load_wr(g):
             wr_sb[g] = keep.tile([P, 2 * D], U8, name="wr%d" % g, align_bytes=64)
@@ -89,80 +87,79 @@ def tile_shared_routed_expert_pair_s1_kernel(tc, h, v, r, x, ws, wr_words, wr_sc
             free_banks.remove(b)
             return b
 
-        ordered, turned, grouped, lhs, ws_grouped, ws_q, acc = {}, {}, {}, {}, {}, {}, {}
+        ordered, turned, grouped, lhs, ws_grouped, ws_q, acc, y_sb = {}, {}, {}, {}, {}, {}, {}, {}
+        both_spans = (0, 1)
 
-        def sort(*keys, on_scalar=False):
-            for key in keys:
-                width = raw[key].shape[1]
-                ordered[key] = stage.tile([P, 2, width // 2], BF16, name="ordered")
-                dst = ordered[key][:].rearrange("p u (w e) -> p u w e", e=2)
-                src = raw[key][:].rearrange("p (w u e) -> p u w e", u=2, e=2)
-                if key[0] == "v":
-                    i = key[1]
+        def sort(sheet, spans=both_spans, on_scalar=False):
+            width = len(spans) * SPAN
+            rows = sheet_sb[sheet][:, spans[0] * SPAN : spans[0] * SPAN + width]
+            tile = stage.tile([P, 2, width // 2], BF16, name="ordered")
+            kind, i = sheet
+            if on_scalar:
+                words = rows.bitcast(F32).rearrange("p (w u) -> p u w", u=2)
+                nc.scalar.copy(out=tile[:].bitcast(F32), in_=words)
+            else:
+                dst = tile[:].rearrange("p u (w e) -> p u w e", e=2)
+                src = rows.rearrange("p (w u e) -> p u w e", u=2, e=2)
+                if kind == "v":
                     nc.vector.tensor_scalar(
                         out=dst, in0=src, scalar1=r_sb[:, i : i + 1], scalar2=None, op0=mybir.AluOpType.mult
                     )
-                elif on_scalar:
-                    words = raw[key][:].bitcast(F32).rearrange("p (w u) -> p u w", u=2)
-                    nc.scalar.copy(out=ordered[key][:].bitcast(F32), in_=words)
                 else:
                     nc.vector.tensor_copy(out=dst, in_=src)
+            for c, s in enumerate(spans):
+                ordered[sheet, s] = tile[:].bitcast(F32)[:, :, c * SPAN_PASSES * P : (c + 1) * SPAN_PASSES * P]
 
-        def turn(*keys):
-            for key in keys:
-                words = ordered[key][:].bitcast(F32)
-                turned[key] = []
-                for s in range(raw[key].shape[1] // SPAN):
-                    b = take_bank()
-                    bank = psum.tile([P, SPAN_PASSES, 2, P], F32, name="turned", tag="bank%d" % b)
-                    for j in range(SPAN_PASSES):
-                        g = s * SPAN_PASSES + j
-                        for u in range(2):
-                            nc.tensor.transpose(bank[:, j, u, :], words[:, u, g * P : (g + 1) * P], ident[:])
-                    turned[key].append((b, bank))
+        def turn(sheet, spans=both_spans):
+            for s in spans:
+                b = take_bank()
+                bank = psum.tile([P, SPAN_PASSES, 2, P], F32, name="turned", tag="bank%d" % b)
+                for j in range(SPAN_PASSES):
+                    for u in range(2):
+                        nc.tensor.transpose(bank[:, j, u, :], ordered[sheet, s][:, u, j * P : (j + 1) * P], ident[:])
+                turned[sheet, s] = (b, bank)
 
-        def regroup(*keys):
-            for key in keys:
-                grouped[key] = stage.tile([P, raw[key].shape[1]], BF16, name="grouped", align_bytes=64)
-                words = grouped[key][:].bitcast(F32).rearrange("p (g t u) -> p g t u", t=P, u=2)
-                for s, (b, bank) in enumerate(turned[key]):
-                    dst = words[:, s * SPAN_PASSES : (s + 1) * SPAN_PASSES, :, :]
-                    nc.scalar.copy(out=dst, in_=bank[:].rearrange("p g u t -> p g t u"))
-                    free_banks.append(b)
+        def regroup(sheet, spans=both_spans):
+            if sheet not in grouped:
+                grouped[sheet] = stage.tile([P, 2 * SPAN], BF16, name="grouped", align_bytes=64)
+            for s in spans:
+                b, bank = turned[sheet, s]
+                words = grouped[sheet][:, s * SPAN : (s + 1) * SPAN].bitcast(F32)
+                dst = words.rearrange("p (j t u) -> p j t u", t=P, u=2)
+                nc.scalar.copy(out=dst, in_=bank[:].rearrange("p j u t -> p j t u"))
+                free_banks.append(b)
 
         def quantize(name, src):
             width = src.shape[1] // PACK
             codes = keep.tile([P, width], U32, name=name + "_codes", align_bytes=64)
             scales = keep.tile([P, width], U8, name=name + "_scales", align_bytes=64)
-            nc.vector.quantize_mx(out=codes[:].bitcast(FP8X4), scales=scales[:], in_=src[:])
+            nc.vector.quantize_mx(out=codes[:].bitcast(FP8X4), scales=scales[:], in_=src)
             return codes, scales
 
-        def quant(key, spans=None):
-            kind, i, first = key
-            if spans is None:
-                spans = range(raw[key].shape[1] // SPAN)
-            src = grouped[key][:, spans[0] * SPAN : (spans[-1] + 1) * SPAN]
-            codes, scales = quantize("%s%d_%d" % (kind, i, first + spans[0]), src)
-            for c in range(codes.shape[1] // P):
+        def quant(sheet, spans=both_spans):
+            kind, i = sheet
+            src = grouped[sheet][:, spans[0] * SPAN : (spans[-1] + 1) * SPAN]
+            codes, scales = quantize("%s%d_%d" % (kind, i, spans[0]), src)
+            for c in range(len(spans) * SPAN_PASSES):
                 cols = slice(c * P, (c + 1) * P)
-                g = (first + spans[0]) * SPAN_PASSES + c
+                g = spans[0] * SPAN_PASSES + c
                 where = (kind, i, g) if kind == "v" else (kind, i + g // PASSES_S, g % PASSES_S)
                 lhs[where] = (codes[:, cols].bitcast(FP8X4), scales[:, cols])
 
-        def group_ws(engine_copy, g, n, first, last):
-            if (g, n) not in ws_grouped:
-                ws_grouped[g, n] = keep.tile([P, PACK * N_TILE], BF16, name="wsg%d_%d" % (g, n), align_bytes=64)
+        def group_ws(g, n, cut):
+            ws_grouped[g, n] = keep.tile([P, PACK * N_TILE], BF16, name="wsg%d_%d" % (g, n), align_bytes=64)
             dst = ws_grouped[g, n][:].rearrange("p (c i j) -> p c j i", i=RUN, j=PACK)
             src = ws_raw[g, n][:].rearrange("p j (c i) -> p c j i", i=RUN)
-            runs = slice(first // RUN, last // RUN)
-            engine_copy(out=dst[:, runs, :, :], in_=src[:, runs, :, :])
+            return [(dst[:, : cut // RUN], src[:, : cut // RUN]), (dst[:, cut // RUN :], src[:, cut // RUN :])]
 
-        def group_ws_shared(g, n):
-            group_ws(nc.scalar.copy, g, n, 0, WS_CUT)
-            group_ws(nc.vector.tensor_copy, g, n, WS_CUT, N_TILE)
+        def scalar_share(shares):
+            nc.scalar.copy(out=shares[0][0], in_=shares[0][1])
+
+        def vector_share(shares):
+            nc.vector.tensor_copy(out=shares[1][0], in_=shares[1][1])
 
         def quant_ws(g, n):
-            ws_q[g, n] = quantize("ws%d_%d" % (g, n), ws_grouped[g, n])
+            ws_q[g, n] = quantize("ws%d_%d" % (g, n), ws_grouped[g, n][:])
 
         def routed(i, cols, passes=range(PASSES_R)):
             first, width = cols
@@ -201,83 +198,107 @@ def tile_shared_routed_expert_pair_s1_kernel(tc, h, v, r, x, ws, wr_words, wr_sc
             first, width = cols
             n, within = divmod(first, N_TILE)
             b, bank = acc[i, cols]
-            y = keep.tile([P, width], F32, name="y%d_%d" % (i, first))
+            if i not in y_sb:
+                y_sb[i] = keep.tile([P, D], F32, name="y%d" % i)
             nc.vector.tensor_tensor(
-                out=y[:], in0=bank[:], in1=x_sb[i, n][:, within : within + width], op=mybir.AluOpType.add
+                out=y_sb[i][:, first : first + width],
+                in0=bank[:],
+                in1=x_sb[i, n][:, within : within + width],
+                op=mybir.AluOpType.add,
             )
             free_banks.append(b)
-            nc.sync.dma_start(out=out_rows[:, i, first : first + width], in_=y[:])
+
+        def store(i, cols):
+            first, width = cols
+            nc.sync.dma_start(out=out_rows[:, i, first : first + width], in_=y_sb[i][:, first : first + width])
 
         def both(i, cols):
             routed(i, cols)
             shared(i, cols)
 
-        left, right = (0, N_TILE), (N_TILE, N_TILE)
+        warm_codes, warm_scales = quantize("warm", warm_in[:])
+        nc.vector.memset(wr_sc[:].rearrange("p g n -> p (g n)").bitcast(I32), 0)
+        warm_acc = psum.tile([P, P], F32, name="warm_acc", tag="bank%d" % (BANKS - 1))
+
+        def warm(count):
+            for c in range(count):
+                nc.tensor.matmul_mx(
+                    out=warm_acc[:],
+                    lhsT=warm_codes[:].bitcast(FP8X4),
+                    lhsT_scale=warm_scales[:],
+                    rhs=warm_codes[:].bitcast(FP8X4),
+                    rhs_scale=warm_scales[:],
+                    start=(c == 0),
+                    stop=(c == count - 1),
+                )
+
+        left, right, whole = (0, N_TILE), (N_TILE, N_TILE), (0, D)
+        v_of = [("v", i) for i in range(TILES)]
+        h_of = [("h", i) for i in range(TILES)]
 
         nc.sync.dma_start(out=r_sb[:], in_=r.rearrange("(p i) -> p i", i=TILES))
-        early = [("v", i, s) for s in range(2) for i in range(2)]
-        for kind, i, s in early:
-            load_v(i, s, 1)
+        for i in range(3):
+            load_v(i)
         load_wr_scales()
         load_wr(0)
         load_wr(1)
         load_ws(0, 0)
         load_wr(2)
-        load_v(2)
-        load_wr(3)
         load_h(0)
+        load_wr(3)
         load_ws(1, 0)
         load_v(3)
-        load_x(0, 2, [0])
+        load_x(0, 2, left)
         load_h(2)
         load_v(4)
-        load_x(2, 4, [0])
+        load_x(2, 2, left)
         load_h(4)
         load_ws(0, 1)
-        load_v(5)
         load_ws(1, 1)
-        load_x(0, 6, [1])
+        load_v(5)
+        load_x(0, 4, right)
+        load_x(4, 2, whole)
         load_v(6)
         load_h(6)
         load_v(7)
-        load_x(6, 2, [0, 1])
+        load_x(6, 2, whole)
 
-        v_of = [("v", i, 0) for i in range(TILES)]
-        h_of = [("h", i, 0) for i in range(TILES)]
-        half = N_TILE // 2
-
-        sort(*early)
-        turn(*early)
-        regroup(*early)
-        for key in early:
-            quant(key)
-        group_ws(nc.scalar.copy, 0, 0, 0, N_TILE)
-        sort(v_of[2])
-        quant_ws(0, 0)
+        warm(20)
+        for i in range(3):
+            sort(v_of[i], [0])
+            sort(v_of[i], [1])
+            turn(v_of[i])
+            if i < 2:
+                warm(7)
+            regroup(v_of[i])
+        for i in range(3):
+            quant(v_of[i], [0])
+            quant(v_of[i], [1])
+        shares = group_ws(0, 0, 384)
+        scalar_share(shares)
+        vector_share(shares)
         sort(h_of[0])
-        for g in range(PASSES_R):
-            if g == PASSES_R - 1:
-                turn(v_of[2])
-                regroup(v_of[2])
-            for i in range(2):
-                routed(i, left, [g])
-                routed(i, right, [g])
-        turn(h_of[0])
-        quant(v_of[2], [0])
-        quant(v_of[2], [1])
-        group_ws(nc.scalar.copy, 1, 0, 0, WS_CUT)
-        group_ws(nc.vector.tensor_copy, 1, 0, WS_CUT, N_TILE)
+        quant_ws(0, 0)
+        for tiles, passes in [((0, 1), [0]), ((0, 1), [1]), ((2,), [0, 1]), ((0, 1, 2), [2]), ((0, 1, 2), [3])]:
+            if passes == [3]:
+                turn(h_of[0])
+            for i in tiles:
+                routed(i, left, passes)
+                routed(i, right, passes)
+        shares = group_ws(1, 0, 128)
+        vector_share(shares)
+        scalar_share(shares)
         regroup(h_of[0])
-        routed(2, left)
-        routed(2, right)
-        sort(v_of[3])
-        quant(h_of[0])
-        sort(h_of[2], on_scalar=True)
+        sort(v_of[3], [0])
+        sort(v_of[3], [1])
+        quant(h_of[0], [0])
         quant_ws(1, 0)
+        quant(h_of[0], [1])
         turn(v_of[3])
         regroup(v_of[3])
         shared(0, left)
         shared(1, left)
+        sort(h_of[2])
         quant(v_of[3], [0])
         add_x(0, left)
         quant(v_of[3], [1])
@@ -293,55 +314,64 @@ def tile_shared_routed_expert_pair_s1_kernel(tc, h, v, r, x, ws, wr_words, wr_sc
         regroup(v_of[4])
         shared(2, left)
         shared(3, left)
-        group_ws(nc.vector.tensor_copy, 0, 1, half, N_TILE)
+        shares = group_ws(0, 1, 256)
+        vector_share(shares)
         quant(v_of[4], [0])
         add_x(2, left)
         quant(v_of[4], [1])
         turn(h_of[4])
         regroup(h_of[4])
         routed(4, left)
-        sort(v_of[5])
-        group_ws(nc.scalar.copy, 0, 1, 0, half)
+        scalar_share(shares)
         add_x(3, left)
+        shares = group_ws(1, 1, 256)
+        routed(3, right)
+        sort(v_of[5])
+        quant(h_of[4])
+        vector_share(shares)
+        scalar_share(shares)
+        quant_ws(0, 1)
+        shared(4, left)
+        routed(4, right)
+        quant_ws(1, 1)
         turn(v_of[5])
         regroup(v_of[5])
-        quant(h_of[4])
-        routed(3, right)
-        quant_ws(0, 1)
-        group_ws(nc.scalar.copy, 1, 1, 0, N_TILE - WS_CUT)
-        group_ws(nc.vector.tensor_copy, 1, 1, N_TILE - WS_CUT, N_TILE)
-        shared(4, left)
-        quant(v_of[5])
-        routed(4, right)
         add_x(4, left)
         sort(v_of[6])
-        quant_ws(1, 1)
-        both(5, left)
-        sort(h_of[6], on_scalar=True)
         for i in range(5):
             shared(i, right)
-        add_x(5, left)
+        sort(h_of[6], on_scalar=True)
+        quant(v_of[5])
         add_x(0, right)
-        add_x(1, right)
-        turn(v_of[6], h_of[6])
-        regroup(v_of[6], h_of[6])
-        add_x(2, right)
+        store(0, whole)
         sort(v_of[7])
-        both(5, right)
-        quant(v_of[6], [0])
-        quant(v_of[6], [1])
-        add_x(3, right)
-        quant(h_of[6])
-        add_x(4, right)
+        both(5, left)
+        for i in range(1, 4):
+            add_x(i, right)
+            store(i, whole)
+        turn(v_of[6])
+        turn(h_of[6])
+        regroup(v_of[6])
         turn(v_of[7])
+        regroup(h_of[6])
         regroup(v_of[7])
-        add_x(5, right)
+        add_x(4, right)
+        store(4, whole)
+        both(5, right)
+        add_x(5, left)
+        quant(v_of[6])
+        quant(h_of[6])
         both(6, left)
+        add_x(5, right)
+        store(5, whole)
         quant(v_of[7])
         add_x(6, left)
+        store(6, left)
         for i, cols in [(6, right), (7, left)]:
             both(i, cols)
             add_x(i, cols)
+            store(i, cols)
         for first in range(N_TILE, D, P):
             both(7, (first, P))
             add_x(7, (first, P))
+            store(7, (first, P))

@@ -44,9 +44,6 @@ def tile_shared_routed_expert_pair_s1_kernel(tc, h, v, r, x, ws, wr_words, wr_sc
         make_identity(nc, ident[:])
 
         wr_sc = keep.tile([P, PASSES_R, D], U8, name="wr_sc", align_bytes=64)
-        warm_in = keep.tile([P, K_PASS], BF16, name="warm_in", align_bytes=64)
-        nc.vector.memset(warm_in[:], 1.0)
-
         r_sb = keep.tile([P, TILES], BF16, name="r_sb")
         sheet_sb, x_sb, wr_sb, ws_raw = {}, {}, {}, {}
 
@@ -216,21 +213,7 @@ def tile_shared_routed_expert_pair_s1_kernel(tc, h, v, r, x, ws, wr_words, wr_sc
             routed(i, cols)
             shared(i, cols)
 
-        warm_codes, warm_scales = quantize("warm", warm_in[:])
         nc.vector.memset(wr_sc[:].rearrange("p g n -> p (g n)").bitcast(I32), 0)
-        warm_acc = psum.tile([P, P], F32, name="warm_acc", tag="bank%d" % (BANKS - 1))
-
-        def warm(count):
-            for c in range(count):
-                nc.tensor.matmul_mx(
-                    out=warm_acc[:],
-                    lhsT=warm_codes[:].bitcast(FP8X4),
-                    lhsT_scale=warm_scales[:],
-                    rhs=warm_codes[:].bitcast(FP8X4),
-                    rhs_scale=warm_scales[:],
-                    start=(c == 0),
-                    stop=(c == count - 1),
-                )
 
         left, right, whole = (0, N_TILE), (N_TILE, N_TILE), (0, D)
         v_of = [("v", i) for i in range(TILES)]
@@ -263,13 +246,10 @@ def tile_shared_routed_expert_pair_s1_kernel(tc, h, v, r, x, ws, wr_words, wr_sc
         load_v(7)
         load_x(6, 2, whole)
 
-        warm(20)
         for i in range(3):
             sort(v_of[i], [0])
             sort(v_of[i], [1])
             turn(v_of[i])
-            if i < 2:
-                warm(7)
             regroup(v_of[i])
         for i in range(3):
             quant(v_of[i], [0])

from contextlib import ExitStack

import concourse.mybir as mybir
from concourse.masks import make_identity

M, F, E, D = 1024, 1024, 2048, 1024
FLOPS = 2 * M * D * (F + E)

F32 = mybir.dt.float32
BF16 = mybir.dt.bfloat16
I32 = mybir.dt.int32
U32 = mybir.dt.uint32
U8 = mybir.dt.uint8
FP8X4 = mybir.dt.float8_e4m3fn_x4
FP4X4 = mybir.dt.float4_e2m1fn_x4

P = 128
PACK = 4
K_PASS = P * PACK
TILES = M // P
N_TILE = 512
PASSES_S = F // K_PASS
PASSES_R = E // K_PASS
SPAN = 1024
SPAN_PASSES = SPAN // K_PASS
BANKS = 8
RUN = 4


def tile_shared_routed_expert_pair_s1_kernel(tc, h, v, r, x, ws, wr_words, wr_scales, out):
    nc = tc.nc
    h_rows = h.rearrange("(p i) k -> p i k", i=TILES)
    v_rows = v.rearrange("(p i) k -> p i k", i=TILES)
    x_rows = x.rearrange("(p i) n -> p i n", i=TILES)
    out_rows = out.rearrange("(p i) n -> p i n", i=TILES)

    with ExitStack() as ctx:
        keep = ctx.enter_context(tc.tile_pool(name="keep", bufs=1))
        stage = ctx.enter_context(tc.tile_pool(name="stage", bufs=4))
        psum = ctx.enter_context(tc.psum_pool(name="psum", bufs=1))
        ctx.enter_context(tc.manual_schedule())

        ident = keep.tile([P, P], F32, name="ident")
        make_identity(nc, ident[:])

        wr_sc = keep.tile([P, PASSES_R, D], U8, name="wr_sc", align_bytes=64)
        r_sb = keep.tile([P, TILES], BF16, name="r_sb")
        sheet_sb, x_sb, wr_sb, ws_raw = {}, {}, {}, {}

        def load_v(i):
            sheet_sb["v", i] = keep.tile([P, 2 * SPAN], BF16, name="v%d" % i)
            nc.sync.dma_start(out=sheet_sb["v", i][:], in_=v_rows[:, i, :])

        def load_h(i):
            sheet_sb["h", i] = keep.tile([P, 2 * SPAN], BF16, name="h%d" % i)
            nc.sync.dma_start(out=sheet_sb["h", i][:], in_=h_rows[:, i : i + 2, :].rearrange("p i k -> p (i k)"))

        def load_x(first, count, cols):
            start, width = cols
            rows = keep.tile([P, count, width], BF16, name="x%d_%d" % (first, start))
            nc.sync.dma_start(out=rows[:], in_=x_rows[:, first : first + count, start : start + width])
            for c in range(count):
                for j in range(width // N_TILE):
                    x_sb[first + c, start // N_TILE + j] = rows[:, c, j * N_TILE : (j + 1) * N_TILE]

        def load_wr(g):
            wr_sb[g] = keep.tile([P, 2 * D], U8, name="wr%d" % g, align_bytes=64)
            nc.sync.dma_start(out=wr_sb[g][:].bitcast(I32), in_=wr_words[g].bitcast(I32))

        def load_wr_scales():
            by_row = wr_scales.rearrange("g (q s) n -> s q g n", s=4)
            for s in range(4):
                nc.sync.dma_start(out=wr_sc[s:P:32, :, :].bitcast(I32), in_=by_row[s].bitcast(I32))

        def load_ws(g, n):
            ws_raw[g, n] = keep.tile([P, PACK, N_TILE], BF16, name="ws%d_%d" % (g, n))
            src = ws[g * K_PASS : (g + 1) * K_PASS, n * N_TILE : (n + 1) * N_TILE]
            nc.sync.dma_start(out=ws_raw[g, n][:], in_=src.rearrange("(p j) n -> p j n", j=PACK))

        free_banks = list(range(BANKS))

        def take_bank():
            b = free_banks[0]
            free_banks.remove(b)
            return b

        ordered, turned, grouped, lhs, ws_grouped, ws_q, acc, y_sb = {}, {}, {}, {}, {}, {}, {}, {}
        both_spans = (0, 1)

        def sort(sheet, spans=both_spans, on_scalar=False):
            width = len(spans) * SPAN
            rows = sheet_sb[sheet][:, spans[0] * SPAN : spans[0] * SPAN + width]
            tile = stage.tile([P, 2, width // 2], BF16, name="ordered")
            kind, i = sheet
            if on_scalar:
                words = rows.bitcast(F32).rearrange("p (w u) -> p u w", u=2)
                nc.scalar.copy(out=tile[:].bitcast(F32), in_=words)
            else:
                dst = tile[:].rearrange("p u (w e) -> p u w e", e=2)
                src = rows.rearrange("p (w u e) -> p u w e", u=2, e=2)
                if kind == "v":
                    nc.vector.tensor_scalar(
                        out=dst, in0=src, scalar1=r_sb[:, i : i + 1], scalar2=None, op0=mybir.AluOpType.mult
                    )
                else:
                    nc.vector.tensor_copy(out=dst, in_=src)
            for c, s in enumerate(spans):
                ordered[sheet, s] = tile[:].bitcast(F32)[:, :, c * SPAN_PASSES * P : (c + 1) * SPAN_PASSES * P]

        def turn(sheet, spans=both_spans):
            for s in spans:
                b = take_bank()
                bank = psum.tile([P, SPAN_PASSES, 2, P], F32, name="turned", tag="bank%d" % b)
                for j in range(SPAN_PASSES):
                    for u in range(2):
                        nc.tensor.transpose(bank[:, j, u, :], ordered[sheet, s][:, u, j * P : (j + 1) * P], ident[:])
                turned[sheet, s] = (b, bank)

        def regroup(sheet, spans=both_spans):
            if sheet not in grouped:
                grouped[sheet] = stage.tile([P, 2 * SPAN], BF16, name="grouped", align_bytes=64)
            for s in spans:
                b, bank = turned[sheet, s]
                words = grouped[sheet][:, s * SPAN : (s + 1) * SPAN].bitcast(F32)
                dst = words.rearrange("p (j t u) -> p j t u", t=P, u=2)
                nc.scalar.copy(out=dst, in_=bank[:].rearrange("p j u t -> p j t u"))
                free_banks.append(b)

        def quantize(name, src):
            width = src.shape[1] // PACK
            codes = keep.tile([P, width], U32, name=name + "_codes", align_bytes=64)
            scales = keep.tile([P, width], U8, name=name + "_scales", align_bytes=64)
            nc.vector.quantize_mx(out=codes[:].bitcast(FP8X4), scales=scales[:], in_=src)
            return codes, scales

        def quant(sheet, spans=both_spans):
            kind, i = sheet
            src = grouped[sheet][:, spans[0] * SPAN : (spans[-1] + 1) * SPAN]
            codes, scales = quantize("%s%d_%d" % (kind, i, spans[0]), src)
            for c in range(len(spans) * SPAN_PASSES):
                cols = slice(c * P, (c + 1) * P)
                g = spans[0] * SPAN_PASSES + c
                where = (kind, i, g) if kind == "v" else (kind, i + g // PASSES_S, g % PASSES_S)
                lhs[where] = (codes[:, cols].bitcast(FP8X4), scales[:, cols])

        def group_ws(g, n, cut):
            ws_grouped[g, n] = keep.tile([P, PACK * N_TILE], BF16, name="wsg%d_%d" % (g, n), align_bytes=64)
            dst = ws_grouped[g, n][:].rearrange("p (c i j) -> p c j i", i=RUN, j=PACK)
            src = ws_raw[g, n][:].rearrange("p j (c i) -> p c j i", i=RUN)
            return [(dst[:, : cut // RUN], src[:, : cut // RUN]), (dst[:, cut // RUN :], src[:, cut // RUN :])]

        def scalar_share(shares):
            nc.scalar.copy(out=shares[0][0], in_=shares[0][1])

        def vector_share(shares):
            nc.vector.tensor_copy(out=shares[1][0], in_=shares[1][1])

        def quant_ws(g, n):
            ws_q[g, n] = quantize("ws%d_%d" % (g, n), ws_grouped[g, n][:])

        def routed(i, cols, passes=range(PASSES_R)):
            first, width = cols
            for g in passes:
                if g == 0:
                    b = take_bank()
                    acc[i, cols] = (b, psum.tile([P, width], F32, name="acc", tag="bank%d" % b))
                codes, scales = lhs["v", i, g]
                nc.tensor.matmul_mx(
                    out=acc[i, cols][1][:],
                    lhsT=codes,
                    lhsT_scale=scales,
                    rhs=wr_sb[g][:, 2 * first : 2 * (first + width)].bitcast(FP4X4),
                    rhs_scale=wr_sc[:, g, first : first + width],
                    start=(g == 0),
                    stop=False,
                )

        def shared(i, cols):
            first, width = cols
            n, within = divmod(first, N_TILE)
            for g in range(PASSES_S):
                codes, scales = lhs["h", i, g]
                w_codes, w_scales = ws_q[g, n]
                nc.tensor.matmul_mx(
                    out=acc[i, cols][1][:],
                    lhsT=codes,
                    lhsT_scale=scales,
                    rhs=w_codes[:, within : within + width].bitcast(FP8X4),
                    rhs_scale=w_scales[:, within : within + width],
                    start=False,
                    stop=(g == PASSES_S - 1),
                )

        def add_x(i, cols):
            first, width = cols
            n, within = divmod(first, N_TILE)
            b, bank = acc[i, cols]
            if i not in y_sb:
                y_sb[i] = keep.tile([P, D], F32, name="y%d" % i)
            nc.vector.tensor_tensor(
                out=y_sb[i][:, first : first + width],
                in0=bank[:],
                in1=x_sb[i, n][:, within : within + width],
                op=mybir.AluOpType.add,
            )
            free_banks.append(b)

        def store(i, cols):
            first, width = cols
            nc.sync.dma_start(out=out_rows[:, i, first : first + width], in_=y_sb[i][:, first : first + width])

        def both(i, cols):
            routed(i, cols)
            shared(i, cols)

        nc.vector.memset(wr_sc[:].rearrange("p g n -> p (g n)").bitcast(I32), 0)

        left, right, whole = (0, N_TILE), (N_TILE, N_TILE), (0, D)
        v_of = [("v", i) for i in range(TILES)]
        h_of = [("h", i) for i in range(TILES)]

        nc.sync.dma_start(out=r_sb[:], in_=r.rearrange("(p i) -> p i", i=TILES))
        for i in range(3):
            load_v(i)
        load_wr_scales()
        load_wr(0)
        load_wr(1)
        load_ws(0, 0)
        load_wr(2)
        load_h(0)
        load_wr(3)
        load_ws(1, 0)
        load_v(3)
        load_x(0, 2, left)
        load_h(2)
        load_v(4)
        load_x(2, 2, left)
        load_h(4)
        load_ws(0, 1)
        load_ws(1, 1)
        load_v(5)
        load_x(0, 4, right)
        load_x(4, 2, whole)
        load_v(6)
        load_h(6)
        load_v(7)
        load_x(6, 2, whole)

        for i in range(3):
            sort(v_of[i], [0])
            sort(v_of[i], [1])
            turn(v_of[i])
            regroup(v_of[i])
        for i in range(3):
            quant(v_of[i], [0])
            quant(v_of[i], [1])
        shares = group_ws(0, 0, 384)
        scalar_share(shares)
        vector_share(shares)
        sort(h_of[0])
        quant_ws(0, 0)
        for tiles, passes in [((0, 1), [0]), ((0, 1), [1]), ((2,), [0, 1]), ((0, 1, 2), [2]), ((0, 1, 2), [3])]:
            if passes == [3]:
                turn(h_of[0])
            for i in tiles:
                routed(i, left, passes)
                routed(i, right, passes)
        shares = group_ws(1, 0, 128)
        vector_share(shares)
        scalar_share(shares)
        regroup(h_of[0])
        sort(v_of[3], [0])
        sort(v_of[3], [1])
        quant(h_of[0], [0])
        quant_ws(1, 0)
        quant(h_of[0], [1])
        turn(v_of[3])
        regroup(v_of[3])
        shared(0, left)
        shared(1, left)
        sort(h_of[2])
        quant(v_of[3], [0])
        add_x(0, left)
        quant(v_of[3], [1])
        turn(h_of[2])
        regroup(h_of[2])
        routed(3, left)
        sort(v_of[4])
        add_x(1, left)
        quant(h_of[2], [0])
        quant(h_of[2], [1])
        sort(h_of[4], on_scalar=True)
        turn(v_of[4])
        regroup(v_of[4])
        shared(2, left)
        shared(3, left)
        shares = group_ws(0, 1, 256)
        vector_share(shares)
        quant(v_of[4], [0])
        add_x(2, left)
        quant(v_of[4], [1])
        turn(h_of[4])
        regroup(h_of[4])
        routed(4, left)
        scalar_share(shares)
        add_x(3, left)
        shares = group_ws(1, 1, 256)
        routed(3, right)
        sort(v_of[5])
        quant(h_of[4])
        vector_share(shares)
        scalar_share(shares)
        quant_ws(0, 1)
        shared(4, left)
        routed(4, right)
        quant_ws(1, 1)
        turn(v_of[5])
        regroup(v_of[5])
        add_x(4, left)
        sort(v_of[6])
        for i in range(5):
            shared(i, right)
        sort(h_of[6], on_scalar=True)
        quant(v_of[5])
        add_x(0, right)
        store(0, whole)
        sort(v_of[7])
        both(5, left)
        for i in range(1, 4):
            add_x(i, right)
            store(i, whole)
        turn(v_of[6])
        turn(h_of[6])
        regroup(v_of[6])
        turn(v_of[7])
        regroup(h_of[6])
        regroup(v_of[7])
        add_x(4, right)
        store(4, whole)
        both(5, right)
        add_x(5, left)
        quant(v_of[6])
        quant(h_of[6])
        both(6, left)
        add_x(5, right)
        store(5, whole)
        quant(v_of[7])
        add_x(6, left)
        store(6, left)
        for i, cols in [(6, right), (7, left)]:
            both(i, cols)
            add_x(i, cols)
            store(i, cols)
        for first in range(N_TILE, D, P):
            both(7, (first, P))
            add_x(7, (first, P))
            store(7, (first, P))
